import numpy as np
import ml_dtypes


def mxq(x, axis, fmt="e4m3"):
    dtype, down = {"e4m3": (ml_dtypes.float8_e4m3fn, 7), "e5m2": (ml_dtypes.float8_e5m2, 14)}[fmt]
    v = np.moveaxis(np.asarray(x, np.float32).astype(ml_dtypes.bfloat16).astype(np.float64), axis, -1)
    blocks = v.reshape(v.shape[:-1] + (-1, 32))
    amax = np.abs(blocks).max(-1, keepdims=True)
    byte = np.maximum(np.where(amax > 0, np.frexp(amax)[1] - 1 + 127, 0) - down, 1)
    scale = np.exp2(byte - 127.0)
    codes = (blocks / scale).astype(np.float32).astype(dtype).astype(np.float64)
    return np.moveaxis((codes * scale).reshape(v.shape), -1, axis)


WIDE = False


def mx_kscale(k):
    if not WIDE:
        return np.ones(k)
    levels = np.array([10, -10, 5, -5, 0])
    if k % 512:
        return np.exp2(np.random.permutation(np.resize(levels, k // 32))).repeat(32)
    a = np.empty((k // 512, 16))
    for p in range(k // 512):
        a[p, :8] = np.random.permutation(np.resize(levels, 8))
        for g in range(8):
            far = levels[np.abs(levels - a[p, g]) >= 10]
            a[p, g + 8] = far[np.random.randint(len(far))]
    return np.exp2(a.ravel()).repeat(32)


def f64(x):
    return np.asarray(x).astype(np.float64)


def striped(idx):
    return np.tile(idx.reshape(-1, 16).T, (8, 1)).astype(np.uint16)


def unstriped(offs):
    return offs[:16].T.reshape(-1).astype(np.int64)


def pack_weight(w):
    k, n = w.shape
    w = f64(np.asarray(w, np.float32).astype(ml_dtypes.bfloat16)).reshape(k // 32, 32, n)
    amax = np.abs(w).max(1)
    byte = np.clip(np.where(amax > 0, np.frexp(amax)[1] - 1 + 127 - 7, 1), 1, 254)
    scaled = (w * np.exp2(127.0 - byte)[:, None, :]).reshape(k, n).astype(np.float32)
    words = np.ascontiguousarray(scaled.reshape(k // 512, 128, 4, n).transpose(0, 1, 3, 2)).astype(ml_dtypes.float8_e4m3fn).view(np.uint8)
    return words, np.ascontiguousarray(byte.astype(np.uint8).reshape(k // 512, 16, n))


def unpack_weight(words, scales):
    g, p, n, _ = words.shape
    vals = np.ascontiguousarray(words).view(ml_dtypes.float8_e4m3fn).astype(np.float64) * np.repeat(np.exp2(scales.astype(np.float64) - 127.0), 8, axis=1)[..., None]
    return vals.transpose(0, 1, 3, 2).reshape(g * 512, n)


def relu(v):
    return np.maximum(v, 0.0)


K, T, S, N = 1024, 1024, 512, 512


def setup_inputs():
    n = np.random.standard_normal
    s = mx_kscale(K)[:, None]
    words, scales = pack_weight(n((K, N)) / np.sqrt(K) / s)
    return {
        "xT": (n((K, S)) * s).astype(np.float32),
        "w_words": words,
        "w_scales": scales,
        "b": (0.3 * n((N, 1))).astype(np.float32),
        "gate": np.tile(np.random.uniform(0.2, 1.0, S), (N, 1)).astype(np.float32),
        "offs": striped(np.random.permutation(T)[:S]),
    }


def reference(xT, w_words, w_scales, b, gate, offs):
    w = unpack_weight(w_words, w_scales)
    idx = unstriped(offs)
    xq = mxq(f64(xT), 0, "e4m3")
    y = w.T @ xq
    y = relu(y + f64(b))
    out = np.zeros((N, T))
    out[:, idx] = f64(gate) * y
    return out

@@ -1,0 +1,133 @@
+from contextlib import ExitStack
+
+import concourse.mybir as mybir
+
+K, T, S, N = 1024, 1024, 512, 512
+FLOPS = 2 * K * S * N
+
+F32 = mybir.dt.float32
+BF16 = mybir.dt.bfloat16
+I32 = mybir.dt.int32
+U32 = mybir.dt.uint32
+U16 = mybir.dt.uint16
+U8 = mybir.dt.uint8
+FP8X4 = mybir.dt.float8_e4m3fn_x4
+RELU = mybir.ActivationFunctionType.Relu
+MULT = mybir.AluOpType.mult
+
+P = 128
+PACK = 4
+K_PASS = P * PACK
+PASSES = K // K_PASS
+BLOCKS = N // P
+CHUNKS = ((0, 256), (256, 256))
+LATE = (3,)
+SCALAR_SHARE = {(0, 0): 96, (0, 1): 96, (1, 0): 256, (1, 1): 96}
+
+
+def tile_picked_place_lin_relu_sub_l_kernel(tc, xT, w_words, w_scales, b, gate, offs, out):
+    nc = tc.nc
+    with ExitStack() as ctx:
+        lists = ctx.enter_context(tc.tile_pool(name="lists", bufs=1))
+        keep = ctx.enter_context(tc.tile_pool(name="keep", bufs=1))
+        psum = ctx.enter_context(tc.psum_pool(name="psum", bufs=1))
+
+        offsets = lists.tile([P, S // 16], U16, name="offsets")
+        w_codes = keep.tile([P, PASSES, N], U32, name="w_codes", align_bytes=64)
+        w_planes = keep.tile([P, N], U8, name="w_planes", align_bytes=64)
+        bias = keep.tile([P, BLOCKS], F32, name="bias")
+        warm = keep.tile([P, 1], F32, name="warm")
+        gates = [keep.tile([P, S], F32, name=f"gate{m}") for m in range(BLOCKS)]
+        windows = [keep.tile([P, T], F32, name=f"window{m}") for m in range(BLOCKS)]
+        raw = {
+            (c, a): keep.tile([P, PACK, CHUNKS[c][1]], F32, name=f"raw{c}_{a}")
+            for c in range(len(CHUNKS))
+            for a in range(PASSES)
+        }
+
+        nc.vector.memset(w_planes[:].bitcast(I32), 0)
+        nc.vector.memset(warm[:], 0.0)
+
+        def load_x(c, a):
+            c0, n = CHUNKS[c]
+            rows = xT[a * K_PASS : (a + 1) * K_PASS, c0 : c0 + n]
+            nc.sync.dma_start(out=raw[c, a][:], in_=rows.rearrange("(p j) s -> p j s", j=PACK))
+
+        def load_w(a):
+            nc.sync.dma_start(
+                out=w_codes[:, a, :].bitcast(I32), in_=w_words[a].rearrange("p m r -> p (m r)").bitcast(I32)
+            )
+
+        def load_gate(m):
+            nc.sync.dma_start(out=gates[m][:], in_=gate[m * P : (m + 1) * P, :])
+
+        load_x(0, 0)
+        load_w(0)
+        load_x(0, 1)
+        load_w(1)
+        for q in range(4):
+            nc.scalar.dma_start(
+                out=w_planes[32 * q : 32 * q + 8, :].bitcast(I32), in_=w_scales[:, 4 * q : 4 * q + 4, :].bitcast(I32)
+            )
+        with nc.allow_non_contiguous_dma(reason="one bias value a partition"):
+            nc.scalar.dma_start(out=bias[:], in_=b.rearrange("(m p) o -> p (m o)", p=P))
+        nc.sync.dma_start(offsets[:], offs)
+        load_gate(0)
+        load_gate(1)
+        load_gate(2)
+        load_x(1, 0)
+        load_x(1, 1)
+        load_gate(3)
+
+        nc.scalar.activation(warm[:], warm[:], RELU)
+        for m in (0, 1):
+            nc.vector.memset(windows[m][:], 0.0)
+        for m in (2, 3):
+            nc.gpsimd.memset(windows[m][:], 0.0)
+
+        late_y = {m: keep.tile([P, S], F32, name=f"late_y{m}") for m in LATE}
+
+        for c, (c0, n) in enumerate(CHUNKS):
+            acc = [psum.tile([P, n], F32, name=f"acc{c}_{m}") for m in range(BLOCKS)]
+            for a in range(PASSES):
+                grouped = keep.tile([P, n, PACK], BF16, name=f"grouped{c}_{a}", align_bytes=64)
+                share = SCALAR_SHARE[c, a]
+                nc.scalar.copy(
+                    out=grouped[:, 0:share, :], in_=raw[c, a][:, :, 0:share].rearrange("p j s -> p s j")
+                )
+                if share < n:
+                    nc.vector.tensor_copy(
+                        out=grouped[:, share:n, :], in_=raw[c, a][:, :, share:n].rearrange("p j s -> p s j")
+                    )
+                codes = keep.tile([P, n], U32, name=f"codes{c}_{a}", align_bytes=64)
+                plane = keep.tile([P, n], U8, name=f"plane{c}_{a}", align_bytes=64)
+                nc.vector.quantize_mx(
+                    out=codes[:].bitcast(FP8X4), scales=plane[:], in_=grouped[:].rearrange("p s j -> p (s j)")
+                )
+                for m in range(BLOCKS):
+                    cols = slice(m * P, (m + 1) * P)
+                    nc.tensor.matmul_mx(
+                        out=acc[m][:],
+                        lhsT=w_codes[:, a, cols].bitcast(FP8X4),
+                        lhsT_scale=w_planes[4 * a : P, cols],
+                        rhs=codes[:].bitcast(FP8X4),
+                        rhs_scale=plane[:],
+                        start=(a == 0),
+                        stop=(a == PASSES - 1),
+                    )
+            for m in range(BLOCKS):
+                if m in LATE:
+                    nc.scalar.activation(late_y[m][:, c0 : c0 + n], acc[m][:], RELU, bias=bias[:, m : m + 1])
+                    continue
+                y = keep.tile([P, n], F32, name=f"y{c}_{m}")
+                nc.scalar.activation(y[:], acc[m][:], RELU, bias=bias[:, m : m + 1])
+                z = keep.tile([P, n], F32, name=f"z{c}_{m}")
+                nc.vector.tensor_tensor(z[:], y[:], gates[m][:, c0 : c0 + n], MULT)
+                nc.vector.tensor_copy(windows[m][:].indirect(offsets[:, c0 // 16 : (c0 + n) // 16]), z[:])
+                if c == len(CHUNKS) - 1:
+                    nc.sync.dma_start(out=out[m * P : (m + 1) * P, :], in_=windows[m][:])
+        for m in LATE:
+            z = keep.tile([P, S], F32, name=f"late_z{m}")
+            nc.vector.tensor_tensor(z[:], late_y[m][:], gates[m][:], MULT)
+            nc.vector.tensor_copy(windows[m][:].indirect(offsets[:]), z[:])
+            nc.sync.dma_start(out=out[m * P : (m + 1) * P, :], in_=windows[m][:])

@@ -20,9 +20,10 @@ PACK = 4
 K_PASS = P * PACK
 PASSES = K // K_PASS
 BLOCKS = N // P
-CHUNKS = ((0, 256), (256, 256))
-LATE = (3,)
-SCALAR_SHARE = {(0, 0): 96, (0, 1): 96, (1, 0): 256, (1, 1): 96}
+CHUNKS = ((0, 128), (128, 128), (256, 256))
+SCALAR_SHARE = {(0, 0): 32, (0, 1): 32, (1, 0): 128, (1, 1): 128, (2, 0): 256, (2, 1): 256}
+W_PARTS = ((0, 128), (128, 512))
+EARLY = 2
 
 
 def tile_picked_place_lin_relu_sub_l_kernel(tc, xT, w_words, w_scales, b, gate, offs, out):
@@ -30,104 +31,113 @@ def tile_picked_place_lin_relu_sub_l_kernel(tc, xT, w_words, w_scales, b, gate, 
     with ExitStack() as ctx:
         lists = ctx.enter_context(tc.tile_pool(name="lists", bufs=1))
         keep = ctx.enter_context(tc.tile_pool(name="keep", bufs=1))
-        psum = ctx.enter_context(tc.psum_pool(name="psum", bufs=1))
+        psum = ctx.enter_context(tc.psum_pool(name="psum", bufs=2))
 
         offsets = lists.tile([P, S // 16], U16, name="offsets")
-        w_codes = keep.tile([P, PASSES, N], U32, name="w_codes", align_bytes=64)
+        w_codes = [keep.tile([P, PASSES, hi - lo], U32, name=f"w_codes{lo}", align_bytes=64) for lo, hi in W_PARTS]
         w_planes = keep.tile([P, N], U8, name="w_planes", align_bytes=64)
         bias = keep.tile([P, BLOCKS], F32, name="bias")
         warm = keep.tile([P, 1], F32, name="warm")
-        gates = [keep.tile([P, S], F32, name=f"gate{m}") for m in range(BLOCKS)]
         windows = [keep.tile([P, T], F32, name=f"window{m}") for m in range(BLOCKS)]
-        raw = {
-            (c, a): keep.tile([P, PACK, CHUNKS[c][1]], F32, name=f"raw{c}_{a}")
-            for c in range(len(CHUNKS))
-            for a in range(PASSES)
-        }
+        gates = [keep.tile([P, BLOCKS, n], F32, name=f"gate{c}") for c, (c0, n) in enumerate(CHUNKS)]
+        raw = [keep.tile([P, PASSES, PACK, n], F32, name=f"raw{c}") for c, (c0, n) in enumerate(CHUNKS)]
 
         nc.vector.memset(w_planes[:].bitcast(I32), 0)
         nc.vector.memset(warm[:], 0.0)
+        nc.scalar.activation(warm[:], warm[:], RELU)
 
         def load_x(c, a):
             c0, n = CHUNKS[c]
             rows = xT[a * K_PASS : (a + 1) * K_PASS, c0 : c0 + n]
-            nc.sync.dma_start(out=raw[c, a][:], in_=rows.rearrange("(p j) s -> p j s", j=PACK))
+            nc.sync.dma_start(out=raw[c][:, a, :, :], in_=rows.rearrange("(p j) s -> p j s", j=PACK))
 
-        def load_w(a):
-            nc.sync.dma_start(
-                out=w_codes[:, a, :].bitcast(I32), in_=w_words[a].rearrange("p m r -> p (m r)").bitcast(I32)
-            )
+        def load_w(h):
+            lo, hi = W_PARTS[h]
+            part = w_words[:, :, lo:hi, :].rearrange("a p m r -> p a (m r)")
+            nc.sync.dma_start(out=w_codes[h][:].bitcast(I32), in_=part.bitcast(I32))
 
-        def load_gate(m):
-            nc.sync.dma_start(out=gates[m][:], in_=gate[m * P : (m + 1) * P, :])
+        def w_block(a, m):
+            for h, (lo, hi) in enumerate(W_PARTS):
+                if lo <= m * P < hi:
+                    return w_codes[h][:, a, m * P - lo : (m + 1) * P - lo].bitcast(FP8X4)
+
+        def load_gate(c):
+            c0, n = CHUNKS[c]
+            nc.sync.dma_start(out=gates[c][:], in_=gate.rearrange("(m p) s -> p m s", p=P)[:, :, c0 : c0 + n])
 
         load_x(0, 0)
-        load_w(0)
-        load_x(0, 1)
-        load_w(1)
         for q in range(4):
-            nc.scalar.dma_start(
+            nc.sync.dma_start(
                 out=w_planes[32 * q : 32 * q + 8, :].bitcast(I32), in_=w_scales[:, 4 * q : 4 * q + 4, :].bitcast(I32)
             )
-        with nc.allow_non_contiguous_dma(reason="one bias value a partition"):
-            nc.scalar.dma_start(out=bias[:], in_=b.rearrange("(m p) o -> p (m o)", p=P))
-        nc.sync.dma_start(offsets[:], offs)
+        load_x(0, 1)
+        load_w(0)
         load_gate(0)
-        load_gate(1)
-        load_gate(2)
-        load_x(1, 0)
-        load_x(1, 1)
-        load_gate(3)
+        with nc.allow_non_contiguous_dma(reason="one bias value a partition"):
+            nc.sync.dma_start(out=bias[:], in_=b.rearrange("(m p) o -> p (m o)", p=P))
+        nc.sync.dma_start(offsets[:], offs)
+        load_w(1)
+        for c in range(1, len(CHUNKS)):
+            load_x(c, 0)
+            load_x(c, 1)
+            load_gate(c)
 
-        nc.scalar.activation(warm[:], warm[:], RELU)
         for m in (0, 1):
             nc.vector.memset(windows[m][:], 0.0)
         for m in (2, 3):
             nc.gpsimd.memset(windows[m][:], 0.0)
 
-        late_y = {m: keep.tile([P, S], F32, name=f"late_y{m}") for m in LATE}
+        acc = {}
+        results = {}
 
-        for c, (c0, n) in enumerate(CHUNKS):
-            acc = [psum.tile([P, n], F32, name=f"acc{c}_{m}") for m in range(BLOCKS)]
+        def multiply(c):
+            c0, n = CHUNKS[c]
+            grouped = keep.tile([P, PASSES, n, PACK], BF16, name=f"grouped{c}", tag=f"turn{c}", align_bytes=64)
             for a in range(PASSES):
-                grouped = keep.tile([P, n, PACK], BF16, name=f"grouped{c}_{a}", align_bytes=64)
                 share = SCALAR_SHARE[c, a]
-                nc.scalar.copy(
-                    out=grouped[:, 0:share, :], in_=raw[c, a][:, :, 0:share].rearrange("p j s -> p s j")
-                )
+                if share > 0:
+                    nc.scalar.copy(
+                        out=grouped[:, a, 0:share, :], in_=raw[c][:, a, :, 0:share].rearrange("p j s -> p s j")
+                    )
                 if share < n:
                     nc.vector.tensor_copy(
-                        out=grouped[:, share:n, :], in_=raw[c, a][:, :, share:n].rearrange("p j s -> p s j")
+                        out=grouped[:, a, share:n, :], in_=raw[c][:, a, :, share:n].rearrange("p j s -> p s j")
                     )
-                codes = keep.tile([P, n], U32, name=f"codes{c}_{a}", align_bytes=64)
-                plane = keep.tile([P, n], U8, name=f"plane{c}_{a}", align_bytes=64)
-                nc.vector.quantize_mx(
-                    out=codes[:].bitcast(FP8X4), scales=plane[:], in_=grouped[:].rearrange("p s j -> p (s j)")
-                )
-                for m in range(BLOCKS):
-                    cols = slice(m * P, (m + 1) * P)
+            codes = keep.tile([P, PASSES, n], U32, name=f"codes{c}", align_bytes=64)
+            plane = keep.tile([P, PASSES, n], U8, name=f"plane{c}", align_bytes=64)
+            nc.vector.quantize_mx(
+                out=codes[:].rearrange("p a s -> p (a s)").bitcast(FP8X4),
+                scales=plane[:].rearrange("p a s -> p (a s)"),
+                in_=grouped[:].rearrange("p a s j -> p (a s j)"),
+            )
+            for m in range(BLOCKS):
+                acc[c, m] = psum.tile([P, n], F32, name=f"acc{m}")
+                for a in range(PASSES):
                     nc.tensor.matmul_mx(
-                        out=acc[m][:],
-                        lhsT=w_codes[:, a, cols].bitcast(FP8X4),
-                        lhsT_scale=w_planes[4 * a : P, cols],
-                        rhs=codes[:].bitcast(FP8X4),
-                        rhs_scale=plane[:],
+                        out=acc[c, m][:],
+                        lhsT=w_block(a, m),
+                        lhsT_scale=w_planes[4 * a : P, m * P : (m + 1) * P],
+                        rhs=codes[:, a, :].bitcast(FP8X4),
+                        rhs_scale=plane[:, a, :],
                         start=(a == 0),
                         stop=(a == PASSES - 1),
                     )
-            for m in range(BLOCKS):
-                if m in LATE:
-                    nc.scalar.activation(late_y[m][:, c0 : c0 + n], acc[m][:], RELU, bias=bias[:, m : m + 1])
-                    continue
-                y = keep.tile([P, n], F32, name=f"y{c}_{m}")
-                nc.scalar.activation(y[:], acc[m][:], RELU, bias=bias[:, m : m + 1])
-                z = keep.tile([P, n], F32, name=f"z{c}_{m}")
-                nc.vector.tensor_tensor(z[:], y[:], gates[m][:, c0 : c0 + n], MULT)
-                nc.vector.tensor_copy(windows[m][:].indirect(offsets[:, c0 // 16 : (c0 + n) // 16]), z[:])
+
+        def finish(c, blocks, tag):
+            c0, n = CHUNKS[c]
+            y = keep.tile([P, len(blocks), n], F32, name=f"y{c}_{blocks[0]}", tag=tag, align_bytes=64)
+            for i, m in enumerate(blocks):
+                nc.scalar.activation(y[:, i, :], acc[c, m][:], RELU, bias=bias[:, m : m + 1])
+                nc.vector.tensor_tensor(
+                    windows[m][:].indirect(offsets[:, c0 // 16 : (c0 + n) // 16]), y[:, i, :], gates[c][:, m, :], MULT
+                )
                 if c == len(CHUNKS) - 1:
                     nc.sync.dma_start(out=out[m * P : (m + 1) * P, :], in_=windows[m][:])
-        for m in LATE:
-            z = keep.tile([P, S], F32, name=f"late_z{m}")
-            nc.vector.tensor_tensor(z[:], late_y[m][:], gates[m][:], MULT)
-            nc.vector.tensor_copy(windows[m][:].indirect(offsets[:]), z[:])
-            nc.sync.dma_start(out=out[m * P : (m + 1) * P, :], in_=windows[m][:])
+
+        early, late = list(range(EARLY)), list(range(EARLY, BLOCKS))
+        multiply(0)
+        for c in range(len(CHUNKS)):
+            finish(c, early, f"early{c}")
+            if c + 1 < len(CHUNKS):
+                multiply(c + 1)
+            finish(c, late, f"turn{c + 1}")

@@ -1,6 +1,7 @@
 from contextlib import ExitStack
 
 import concourse.mybir as mybir
+from concourse.masks import make_identity
 
 K, T, S, N = 1024, 1024, 512, 512
 FLOPS = 2 * K * S * N
@@ -22,8 +23,9 @@ PASSES = K // K_PASS
 BLOCKS = N // P
 CHUNKS = ((0, 128), (128, 128), (256, 256))
 SCALAR_SHARE = {(0, 0): 32, (0, 1): 32, (1, 0): 128, (1, 1): 128, (2, 0): 256, (2, 1): 256}
-W_PARTS = ((0, 128), (128, 512))
-EARLY = 2
+GATE_PARTS = ((0, 256), (256, 256))
+W_PARTS = ((0, 512),)
+EARLY = (2, 2, 4)
 
 
 def tile_picked_place_lin_relu_sub_l_kernel(tc, xT, w_words, w_scales, b, gate, offs, out):
@@ -38,12 +40,17 @@ def tile_picked_place_lin_relu_sub_l_kernel(tc, xT, w_words, w_scales, b, gate, 
         w_planes = keep.tile([P, N], U8, name="w_planes", align_bytes=64)
         bias = keep.tile([P, BLOCKS], F32, name="bias")
         warm = keep.tile([P, 1], F32, name="warm")
-        windows = [keep.tile([P, T], F32, name=f"window{m}") for m in range(BLOCKS)]
-        gates = [keep.tile([P, BLOCKS, n], F32, name=f"gate{c}") for c, (c0, n) in enumerate(CHUNKS)]
+        windows = {m: keep.tile([P, T], F32, name=f"window{m}") for m in (0, 1, 3)}
+        gates = [keep.tile([P, BLOCKS, n], F32, name=f"gate{g}") for g, (g0, n) in enumerate(GATE_PARTS)]
         raw = [keep.tile([P, PASSES, PACK, n], F32, name=f"raw{c}") for c, (c0, n) in enumerate(CHUNKS)]
 
-        nc.vector.memset(w_planes[:].bitcast(I32), 0)
+        nc.gpsimd.memset(w_planes[:].bitcast(I32), 0)
         nc.vector.memset(warm[:], 0.0)
+        bias_rows = keep.tile([P, P], F32, name="bias_rows")
+        identity = keep.tile([P, P], F32, name="identity")
+        nc.gpsimd.memset(bias_rows[:], 0.0)
+        nc.gpsimd.dma_start(out=bias_rows[0:BLOCKS, :], in_=b.rearrange("(m p) o -> m (p o)", p=P))
+        make_identity(nc, identity[:])
         nc.scalar.activation(warm[:], warm[:], RELU)
 
         def load_x(c, a):
@@ -61,64 +68,73 @@ def tile_picked_place_lin_relu_sub_l_kernel(tc, xT, w_words, w_scales, b, gate, 
                 if lo <= m * P < hi:
                     return w_codes[h][:, a, m * P - lo : (m + 1) * P - lo].bitcast(FP8X4)
 
-        def load_gate(c):
+        def load_gate(g):
+            g0, n = GATE_PARTS[g]
+            nc.sync.dma_start(out=gates[g][:], in_=gate.rearrange("(m p) s -> p m s", p=P)[:, :, g0 : g0 + n])
+
+        def gate_of(c, m):
             c0, n = CHUNKS[c]
-            nc.sync.dma_start(out=gates[c][:], in_=gate.rearrange("(m p) s -> p m s", p=P)[:, :, c0 : c0 + n])
+            for g, (g0, width) in enumerate(GATE_PARTS):
+                if g0 <= c0 < g0 + width:
+                    return gates[g][:, m, c0 - g0 : c0 - g0 + n]
 
         load_x(0, 0)
+        load_x(0, 1)
         for q in range(4):
             nc.sync.dma_start(
                 out=w_planes[32 * q : 32 * q + 8, :].bitcast(I32), in_=w_scales[:, 4 * q : 4 * q + 4, :].bitcast(I32)
             )
-        load_x(0, 1)
         load_w(0)
         load_gate(0)
-        with nc.allow_non_contiguous_dma(reason="one bias value a partition"):
-            nc.sync.dma_start(out=bias[:], in_=b.rearrange("(m p) o -> p (m o)", p=P))
         nc.sync.dma_start(offsets[:], offs)
-        load_w(1)
-        for c in range(1, len(CHUNKS)):
-            load_x(c, 0)
-            load_x(c, 1)
-            load_gate(c)
+        load_x(1, 0)
+        load_x(1, 1)
+        load_x(2, 0)
+        load_x(2, 1)
+        load_gate(1)
 
         for m in (0, 1):
             nc.vector.memset(windows[m][:], 0.0)
-        for m in (2, 3):
+        for m in (3,):
             nc.gpsimd.memset(windows[m][:], 0.0)
+
+        turned = psum.tile([P, P], F32, name="turned", tag="acc3")
+        nc.tensor.transpose(turned[:], bias_rows[:], identity[:])
+        nc.scalar.copy(out=bias[:], in_=turned[:, 0:BLOCKS])
 
         acc = {}
         results = {}
 
+        def interleave(copy, c, a, grouped, lo, hi):
+            if lo < hi:
+                copy(
+                    out=grouped[:, a, lo:hi, :].rearrange("p (s i) j -> p s j i", i=4),
+                    in_=raw[c][:, a, :, lo:hi].rearrange("p j (s i) -> p s j i", i=4),
+                )
+
         def multiply(c):
             c0, n = CHUNKS[c]
             grouped = keep.tile([P, PASSES, n, PACK], BF16, name=f"grouped{c}", tag=f"turn{c}", align_bytes=64)
-            for a in range(PASSES):
-                share = SCALAR_SHARE[c, a]
-                if share > 0:
-                    nc.scalar.copy(
-                        out=grouped[:, a, 0:share, :], in_=raw[c][:, a, :, 0:share].rearrange("p j s -> p s j")
-                    )
-                if share < n:
-                    nc.vector.tensor_copy(
-                        out=grouped[:, a, share:n, :], in_=raw[c][:, a, :, share:n].rearrange("p j s -> p s j")
-                    )
-            codes = keep.tile([P, PASSES, n], U32, name=f"codes{c}", align_bytes=64)
-            plane = keep.tile([P, PASSES, n], U8, name=f"plane{c}", align_bytes=64)
-            nc.vector.quantize_mx(
-                out=codes[:].rearrange("p a s -> p (a s)").bitcast(FP8X4),
-                scales=plane[:].rearrange("p a s -> p (a s)"),
-                in_=grouped[:].rearrange("p a s j -> p (a s j)"),
-            )
             for m in range(BLOCKS):
                 acc[c, m] = psum.tile([P, n], F32, name=f"acc{m}")
-                for a in range(PASSES):
+            for a in range(PASSES):
+                share = SCALAR_SHARE[c, a]
+                interleave(nc.scalar.copy, c, a, grouped, 0, share)
+                interleave(nc.vector.tensor_copy, c, a, grouped, share, n)
+                codes = keep.tile([P, n], U32, name=f"codes{c}_{a}", align_bytes=64)
+                plane = keep.tile([P, n], U8, name=f"plane{c}_{a}", align_bytes=64)
+                nc.vector.quantize_mx(
+                    out=codes[:].bitcast(FP8X4),
+                    scales=plane[:],
+                    in_=grouped[:, a, :, :].rearrange("p s j -> p (s j)"),
+                )
+                for m in range(BLOCKS):
                     nc.tensor.matmul_mx(
                         out=acc[c, m][:],
                         lhsT=w_block(a, m),
                         lhsT_scale=w_planes[4 * a : P, m * P : (m + 1) * P],
-                        rhs=codes[:, a, :].bitcast(FP8X4),
-                        rhs_scale=plane[:, a, :],
+                        rhs=codes[:].bitcast(FP8X4),
+                        rhs_scale=plane[:],
                         start=(a == 0),
                         stop=(a == PASSES - 1),
                     )
@@ -129,15 +145,16 @@ def tile_picked_place_lin_relu_sub_l_kernel(tc, xT, w_words, w_scales, b, gate, 
             for i, m in enumerate(blocks):
                 nc.scalar.activation(y[:, i, :], acc[c, m][:], RELU, bias=bias[:, m : m + 1])
                 nc.vector.tensor_tensor(
-                    windows[m][:].indirect(offsets[:, c0 // 16 : (c0 + n) // 16]), y[:, i, :], gates[c][:, m, :], MULT
+                    windows[m][:].indirect(offsets[:, c0 // 16 : (c0 + n) // 16]), y[:, i, :], gate_of(c, m), MULT
                 )
                 if c == len(CHUNKS) - 1:
                     nc.sync.dma_start(out=out[m * P : (m + 1) * P, :], in_=windows[m][:])
 
-        early, late = list(range(EARLY)), list(range(EARLY, BLOCKS))
         multiply(0)
+        windows[2] = keep.tile([P, T], F32, name="window2", tag="turn0", align_bytes=64)
+        nc.vector.memset(windows[2][:], 0.0)
         for c in range(len(CHUNKS)):
-            finish(c, early, f"early{c}")
+            finish(c, range(EARLY[c]), f"early{c}")
             if c + 1 < len(CHUNKS):
                 multiply(c + 1)
-            finish(c, late, f"turn{c + 1}")
+                finish(c, range(EARLY[c], BLOCKS), f"turn{c + 1}")

@@ -22,10 +22,8 @@ K_PASS = P * PACK
 PASSES = K // K_PASS
 BLOCKS = N // P
 CHUNKS = ((0, 128), (128, 128), (256, 256))
-SCALAR_SHARE = {(0, 0): 32, (0, 1): 32, (1, 0): 128, (1, 1): 128, (2, 0): 256, (2, 1): 256}
-GATE_PARTS = ((0, 256), (256, 256))
-W_PARTS = ((0, 512),)
-EARLY = (2, 2, 4)
+W_PARTS = ((0, 256), (256, 512))
+GATE_PARTS = ((0, 128, 0, 2), (0, 128, 2, 2), (128, 128, 0, 4), (256, 256, 0, 4))
 
 
 def tile_picked_place_lin_relu_sub_l_kernel(tc, xT, w_words, w_scales, b, gate, offs, out):
@@ -38,123 +36,141 @@ def tile_picked_place_lin_relu_sub_l_kernel(tc, xT, w_words, w_scales, b, gate, 
         offsets = lists.tile([P, S // 16], U16, name="offsets")
         w_codes = [keep.tile([P, PASSES, hi - lo], U32, name=f"w_codes{lo}", align_bytes=64) for lo, hi in W_PARTS]
         w_planes = keep.tile([P, N], U8, name="w_planes", align_bytes=64)
+        bias_rows = keep.tile([P, P], F32, name="bias_rows")
+        identity = keep.tile([P, P], F32, name="identity")
         bias = keep.tile([P, BLOCKS], F32, name="bias")
         warm = keep.tile([P, 1], F32, name="warm")
         windows = {m: keep.tile([P, T], F32, name=f"window{m}") for m in (0, 1, 3)}
-        gates = [keep.tile([P, BLOCKS, n], F32, name=f"gate{g}") for g, (g0, n) in enumerate(GATE_PARTS)]
-        raw = [keep.tile([P, PASSES, PACK, n], F32, name=f"raw{c}") for c, (c0, n) in enumerate(CHUNKS)]
-
-        nc.gpsimd.memset(w_planes[:].bitcast(I32), 0)
-        nc.vector.memset(warm[:], 0.0)
-        bias_rows = keep.tile([P, P], F32, name="bias_rows")
-        identity = keep.tile([P, P], F32, name="identity")
-        nc.gpsimd.memset(bias_rows[:], 0.0)
-        nc.gpsimd.dma_start(out=bias_rows[0:BLOCKS, :], in_=b.rearrange("(m p) o -> m (p o)", p=P))
-        make_identity(nc, identity[:])
-        nc.scalar.activation(warm[:], warm[:], RELU)
+        gates = [keep.tile([P, mn, n], F32, name=f"gate{g}") for g, (g0, n, m0, mn) in enumerate(GATE_PARTS)]
+        raw = {
+            (c, a): keep.tile([P, PACK, n], F32, name=f"raw{c}_{a}", tag=f"raw{c}_{a}", align_bytes=64)
+            for c, (c0, n) in enumerate(CHUNKS)
+            for a in range(PASSES)
+        }
 
         def load_x(c, a):
             c0, n = CHUNKS[c]
             rows = xT[a * K_PASS : (a + 1) * K_PASS, c0 : c0 + n]
-            nc.sync.dma_start(out=raw[c][:, a, :, :], in_=rows.rearrange("(p j) s -> p j s", j=PACK))
+            nc.sync.dma_start(out=raw[c, a][:], in_=rows.rearrange("(p j) s -> p j s", j=PACK))
 
         def load_w(h):
             lo, hi = W_PARTS[h]
             part = w_words[:, :, lo:hi, :].rearrange("a p m r -> p a (m r)")
             nc.sync.dma_start(out=w_codes[h][:].bitcast(I32), in_=part.bitcast(I32))
 
+        def load_w_scales(queue, q):
+            queue.dma_start(
+                out=w_planes[32 * q : 32 * q + 8, :].bitcast(I32), in_=w_scales[:, 4 * q : 4 * q + 4, :].bitcast(I32)
+            )
+
+        def load_gate(g):
+            g0, n, m0, mn = GATE_PARTS[g]
+            rows = gate[m0 * P : (m0 + mn) * P, g0 : g0 + n]
+            nc.sync.dma_start(out=gates[g][:], in_=rows.rearrange("(m p) s -> p m s", p=P))
+
         def w_block(a, m):
             for h, (lo, hi) in enumerate(W_PARTS):
                 if lo <= m * P < hi:
                     return w_codes[h][:, a, m * P - lo : (m + 1) * P - lo].bitcast(FP8X4)
 
-        def load_gate(g):
-            g0, n = GATE_PARTS[g]
-            nc.sync.dma_start(out=gates[g][:], in_=gate.rearrange("(m p) s -> p m s", p=P)[:, :, g0 : g0 + n])
-
         def gate_of(c, m):
             c0, n = CHUNKS[c]
-            for g, (g0, width) in enumerate(GATE_PARTS):
-                if g0 <= c0 < g0 + width:
-                    return gates[g][:, m, c0 - g0 : c0 - g0 + n]
+            for g, (g0, width, m0, mn) in enumerate(GATE_PARTS):
+                if g0 <= c0 < g0 + width and m0 <= m < m0 + mn:
+                    return gates[g][:, m - m0, c0 - g0 : c0 - g0 + n]
 
+        nc.gpsimd.memset(w_planes[:].bitcast(I32), 0)
+        nc.vector.memset(warm[:], 0.0)
+        nc.scalar.activation(warm[:], warm[:], RELU)
+        nc.gpsimd.memset(bias_rows[:], 0.0)
+        nc.gpsimd.dma_start(out=bias_rows[0:BLOCKS, :], in_=b.rearrange("(m p) o -> m (p o)", p=P))
+        make_identity(nc, identity[:])
         load_x(0, 0)
         load_x(0, 1)
         for q in range(4):
-            nc.sync.dma_start(
-                out=w_planes[32 * q : 32 * q + 8, :].bitcast(I32), in_=w_scales[:, 4 * q : 4 * q + 4, :].bitcast(I32)
-            )
+            load_w_scales(nc.sync, q)
         load_w(0)
         load_gate(0)
         nc.sync.dma_start(offsets[:], offs)
+        load_w(1)
+        load_gate(1)
         load_x(1, 0)
         load_x(1, 1)
+        load_gate(2)
         load_x(2, 0)
         load_x(2, 1)
-        load_gate(1)
+        load_gate(3)
 
         for m in (0, 1):
             nc.vector.memset(windows[m][:], 0.0)
-        for m in (3,):
-            nc.gpsimd.memset(windows[m][:], 0.0)
+        nc.gpsimd.memset(windows[3][:], 0.0)
 
+        acc = {}
+        quantised = {}
+
+        def quantise(c, a, grouped_tag, codes_tag):
+            c0, n = CHUNKS[c]
+            grouped = keep.tile([P, n, PACK], BF16, name=f"grouped{c}_{a}", tag=grouped_tag, align_bytes=64)
+            copy = nc.vector.tensor_copy if c == 0 else nc.scalar.copy
+            copy(
+                out=grouped[:].rearrange("p (s i) j -> p s j i", i=4),
+                in_=raw[c, a][:].rearrange("p j (s i) -> p s j i", i=4),
+            )
+            codes = keep.tile([P, n], U32, name=f"codes{c}_{a}", tag=codes_tag, align_bytes=64)
+            plane = keep.tile([P, n], U8, name=f"plane{c}_{a}", align_bytes=64)
+            nc.vector.quantize_mx(
+                out=codes[:].bitcast(FP8X4), scales=plane[:], in_=grouped[:].rearrange("p s j -> p (s j)")
+            )
+            quantised[c, a] = codes, plane
+
+        def multiply(c, a, m):
+            codes, plane = quantised[c, a]
+            if a == 0:
+                acc[c, m] = psum.tile([P, CHUNKS[c][1]], F32, name=f"acc{m}")
+            nc.tensor.matmul_mx(
+                out=acc[c, m][:],
+                lhsT=w_block(a, m),
+                lhsT_scale=w_planes[4 * a : P, m * P : (m + 1) * P],
+                rhs=codes[:].bitcast(FP8X4),
+                rhs_scale=plane[:],
+                start=(a == 0),
+                stop=(a == PASSES - 1),
+            )
+
+        def place(c, m, tag):
+            c0, n = CHUNKS[c]
+            y = keep.tile([P, n], F32, name=f"y{c}_{m}", tag=tag, align_bytes=64)
+            nc.scalar.activation(y[:], acc[c, m][:], RELU, bias=bias[:, m : m + 1])
+            nc.vector.tensor_tensor(
+                windows[m][:].indirect(offsets[:, c0 // 16 : (c0 + n) // 16]), y[:], gate_of(c, m), MULT
+            )
+            if c == len(CHUNKS) - 1:
+                nc.sync.dma_start(out=out[m * P : (m + 1) * P, :], in_=windows[m][:])
+
+        for a in range(PASSES):
+            quantise(0, a, f"grouped0_{a}", f"codes0_{a}")
         turned = psum.tile([P, P], F32, name="turned", tag="acc3")
         nc.tensor.transpose(turned[:], bias_rows[:], identity[:])
         nc.scalar.copy(out=bias[:], in_=turned[:, 0:BLOCKS])
-
-        acc = {}
-        results = {}
-
-        def interleave(copy, c, a, grouped, lo, hi):
-            if lo < hi:
-                copy(
-                    out=grouped[:, a, lo:hi, :].rearrange("p (s i) j -> p s j i", i=4),
-                    in_=raw[c][:, a, :, lo:hi].rearrange("p j (s i) -> p s j i", i=4),
-                )
-
-        def multiply(c):
-            c0, n = CHUNKS[c]
-            grouped = keep.tile([P, PASSES, n, PACK], BF16, name=f"grouped{c}", tag=f"turn{c}", align_bytes=64)
-            for m in range(BLOCKS):
-                acc[c, m] = psum.tile([P, n], F32, name=f"acc{m}")
+        for m in range(BLOCKS):
             for a in range(PASSES):
-                share = SCALAR_SHARE[c, a]
-                interleave(nc.scalar.copy, c, a, grouped, 0, share)
-                interleave(nc.vector.tensor_copy, c, a, grouped, share, n)
-                codes = keep.tile([P, n], U32, name=f"codes{c}_{a}", align_bytes=64)
-                plane = keep.tile([P, n], U8, name=f"plane{c}_{a}", align_bytes=64)
-                nc.vector.quantize_mx(
-                    out=codes[:].bitcast(FP8X4),
-                    scales=plane[:],
-                    in_=grouped[:, a, :, :].rearrange("p s j -> p (s j)"),
-                )
-                for m in range(BLOCKS):
-                    nc.tensor.matmul_mx(
-                        out=acc[c, m][:],
-                        lhsT=w_block(a, m),
-                        lhsT_scale=w_planes[4 * a : P, m * P : (m + 1) * P],
-                        rhs=codes[:].bitcast(FP8X4),
-                        rhs_scale=plane[:],
-                        start=(a == 0),
-                        stop=(a == PASSES - 1),
-                    )
-
-        def finish(c, blocks, tag):
-            c0, n = CHUNKS[c]
-            y = keep.tile([P, len(blocks), n], F32, name=f"y{c}_{blocks[0]}", tag=tag, align_bytes=64)
-            for i, m in enumerate(blocks):
-                nc.scalar.activation(y[:, i, :], acc[c, m][:], RELU, bias=bias[:, m : m + 1])
-                nc.vector.tensor_tensor(
-                    windows[m][:].indirect(offsets[:, c0 // 16 : (c0 + n) // 16]), y[:, i, :], gate_of(c, m), MULT
-                )
-                if c == len(CHUNKS) - 1:
-                    nc.sync.dma_start(out=out[m * P : (m + 1) * P, :], in_=windows[m][:])
-
-        multiply(0)
-        windows[2] = keep.tile([P, T], F32, name="window2", tag="turn0", align_bytes=64)
+                multiply(0, a, m)
+        windows[2] = keep.tile([P, T], F32, name="window2", tag="grouped0_1", align_bytes=64)
         nc.vector.memset(windows[2][:], 0.0)
-        for c in range(len(CHUNKS)):
-            finish(c, range(EARLY[c]), f"early{c}")
-            if c + 1 < len(CHUNKS):
-                multiply(c + 1)
-                finish(c, range(EARLY[c], BLOCKS), f"turn{c + 1}")
+        for m in range(3):
+            place(0, m, f"y0_{m}")
+        for a in range(PASSES):
+            quantise(1, a, f"codes0_{a}", f"codes1_{a}")
+        for m in range(BLOCKS):
+            for a in range(PASSES):
+                multiply(1, a, m)
+        place(0, 3, "raw1_1")
+        for m in (0, 1):
+            place(1, m, f"y1_{m}")
+        for a in range(PASSES):
+            quantise(2, a, f"codes1_{a}", f"codes2_{a}")
+            for m in range(BLOCKS):
+                multiply(2, a, m)
+            place(1, 2 + a, f"raw2_{a}")
+        for m in range(BLOCKS):
+            place(2, m, f"y2_{m}")

@@ -21,9 +21,15 @@ PACK = 4
 K_PASS = P * PACK
 PASSES = K // K_PASS
 BLOCKS = N // P
+QUADRANTS = 4
+SCALE_ROWS = 4
+LIST_ROWS = 16
+NEIGHBOURS = 4
+
 CHUNKS = ((0, 128), (128, 128), (256, 256))
-W_PARTS = ((0, 256), (256, 512))
-GATE_PARTS = ((0, 128, 0, 2), (0, 128, 2, 2), (128, 128, 0, 4), (256, 256, 0, 4))
+LAST = len(CHUNKS) - 1
+HALVES = ((0, 2), (2, 4))
+GATE_PARTS = (HALVES, ((0, 4),), ((0, 4),))
 
 
 def tile_picked_place_lin_relu_sub_l_kernel(tc, xT, w_words, w_scales, b, gate, offs, out):
@@ -33,118 +39,110 @@ def tile_picked_place_lin_relu_sub_l_kernel(tc, xT, w_words, w_scales, b, gate, 
         keep = ctx.enter_context(tc.tile_pool(name="keep", bufs=1))
         psum = ctx.enter_context(tc.psum_pool(name="psum", bufs=2))
 
-        offsets = lists.tile([P, S // 16], U16, name="offsets")
-        w_codes = [keep.tile([P, PASSES, hi - lo], U32, name=f"w_codes{lo}", align_bytes=64) for lo, hi in W_PARTS]
-        w_planes = keep.tile([P, N], U8, name="w_planes", align_bytes=64)
+        offsets = lists.tile([P, S // LIST_ROWS], U16, name="offsets")
+        w_scale_rows = keep.tile([P, N], U8, name="w_scale_rows", align_bytes=64)
         bias_rows = keep.tile([P, P], F32, name="bias_rows")
         identity = keep.tile([P, P], F32, name="identity")
         bias = keep.tile([P, BLOCKS], F32, name="bias")
-        warm = keep.tile([P, 1], F32, name="warm")
+        first_relu = keep.tile([P, 1], F32, name="first_relu")
         windows = {m: keep.tile([P, T], F32, name=f"window{m}") for m in (0, 1, 3)}
-        gates = [keep.tile([P, mn, n], F32, name=f"gate{g}") for g, (g0, n, m0, mn) in enumerate(GATE_PARTS)]
-        raw = {
-            (c, a): keep.tile([P, PACK, n], F32, name=f"raw{c}_{a}", tag=f"raw{c}_{a}", align_bytes=64)
-            for c, (c0, n) in enumerate(CHUNKS)
-            for a in range(PASSES)
-        }
+        w_codes = {}
+        gates = {}
+        raw = {}
+        quantised = {}
+        acc = {}
 
         def load_x(c, a):
-            c0, n = CHUNKS[c]
-            rows = xT[a * K_PASS : (a + 1) * K_PASS, c0 : c0 + n]
+            start, n = CHUNKS[c]
+            rows = xT[a * K_PASS : (a + 1) * K_PASS, start : start + n]
+            raw[c, a] = keep.tile([P, PACK, n], F32, name=f"raw{c}_{a}", tag=f"raw{c}_{a}", align_bytes=64)
             nc.sync.dma_start(out=raw[c, a][:], in_=rows.rearrange("(p j) s -> p j s", j=PACK))
 
-        def load_w(h):
-            lo, hi = W_PARTS[h]
-            part = w_words[:, :, lo:hi, :].rearrange("a p m r -> p a (m r)")
-            nc.sync.dma_start(out=w_codes[h][:].bitcast(I32), in_=part.bitcast(I32))
+        def load_w(lo, hi):
+            words = keep.tile([P, PASSES, (hi - lo) * P], U32, name=f"w_codes{lo}", align_bytes=64)
+            part = w_words[:, :, lo * P : hi * P, :].rearrange("a p m r -> p a (m r)")
+            nc.sync.dma_start(out=words[:].bitcast(I32), in_=part.bitcast(I32))
+            for a in range(PASSES):
+                for m in range(lo, hi):
+                    w_codes[a, m] = words[:, a, (m - lo) * P : (m - lo + 1) * P]
 
-        def load_w_scales(queue, q):
-            queue.dma_start(
-                out=w_planes[32 * q : 32 * q + 8, :].bitcast(I32), in_=w_scales[:, 4 * q : 4 * q + 4, :].bitcast(I32)
+        def load_w_scales(q):
+            rows = w_scales[:, q * SCALE_ROWS : (q + 1) * SCALE_ROWS, :]
+            first = q * (P // QUADRANTS)
+            nc.sync.dma_start(
+                out=w_scale_rows[first : first + PASSES * SCALE_ROWS, :].bitcast(I32), in_=rows.bitcast(I32)
             )
 
-        def load_gate(g):
-            g0, n, m0, mn = GATE_PARTS[g]
-            rows = gate[m0 * P : (m0 + mn) * P, g0 : g0 + n]
-            nc.sync.dma_start(out=gates[g][:], in_=rows.rearrange("(m p) s -> p m s", p=P))
+        def load_gate(c, lo, hi):
+            start, n = CHUNKS[c]
+            part = keep.tile([P, hi - lo, n], F32, name=f"gate{c}_{lo}")
+            rows = gate[lo * P : hi * P, start : start + n]
+            nc.sync.dma_start(out=part[:], in_=rows.rearrange("(m p) s -> p m s", p=P))
+            for m in range(lo, hi):
+                gates[c, m] = part[:, m - lo, :]
 
-        def w_block(a, m):
-            for h, (lo, hi) in enumerate(W_PARTS):
-                if lo <= m * P < hi:
-                    return w_codes[h][:, a, m * P - lo : (m + 1) * P - lo].bitcast(FP8X4)
-
-        def gate_of(c, m):
-            c0, n = CHUNKS[c]
-            for g, (g0, width, m0, mn) in enumerate(GATE_PARTS):
-                if g0 <= c0 < g0 + width and m0 <= m < m0 + mn:
-                    return gates[g][:, m - m0, c0 - g0 : c0 - g0 + n]
-
-        nc.gpsimd.memset(w_planes[:].bitcast(I32), 0)
-        nc.vector.memset(warm[:], 0.0)
-        nc.scalar.activation(warm[:], warm[:], RELU)
+        nc.gpsimd.memset(w_scale_rows[:].bitcast(I32), 0)
+        nc.vector.memset(first_relu[:], 0.0)
+        nc.scalar.activation(first_relu[:], first_relu[:], RELU)
         nc.gpsimd.memset(bias_rows[:], 0.0)
         nc.gpsimd.dma_start(out=bias_rows[0:BLOCKS, :], in_=b.rearrange("(m p) o -> m (p o)", p=P))
         make_identity(nc, identity[:])
-        load_x(0, 0)
-        load_x(0, 1)
-        for q in range(4):
-            load_w_scales(nc.sync, q)
-        load_w(0)
-        load_gate(0)
+
+        for a in range(PASSES):
+            load_x(0, a)
+        for q in range(QUADRANTS):
+            load_w_scales(q)
+        load_w(*HALVES[0])
+        load_gate(0, *HALVES[0])
         nc.sync.dma_start(offsets[:], offs)
-        load_w(1)
-        load_gate(1)
-        load_x(1, 0)
-        load_x(1, 1)
-        load_gate(2)
-        load_x(2, 0)
-        load_x(2, 1)
-        load_gate(3)
+        load_w(*HALVES[1])
+        load_gate(0, *HALVES[1])
+        for c in range(1, len(CHUNKS)):
+            for a in range(PASSES):
+                load_x(c, a)
+            for lo, hi in GATE_PARTS[c]:
+                load_gate(c, lo, hi)
 
         for m in (0, 1):
             nc.vector.memset(windows[m][:], 0.0)
         nc.gpsimd.memset(windows[3][:], 0.0)
 
-        acc = {}
-        quantised = {}
-
         def quantise(c, a, grouped_tag, codes_tag):
-            c0, n = CHUNKS[c]
+            n = CHUNKS[c][1]
             grouped = keep.tile([P, n, PACK], BF16, name=f"grouped{c}_{a}", tag=grouped_tag, align_bytes=64)
             copy = nc.vector.tensor_copy if c == 0 else nc.scalar.copy
             copy(
-                out=grouped[:].rearrange("p (s i) j -> p s j i", i=4),
-                in_=raw[c, a][:].rearrange("p j (s i) -> p s j i", i=4),
+                out=grouped[:].rearrange("p (s i) j -> p s j i", i=NEIGHBOURS),
+                in_=raw[c, a][:].rearrange("p j (s i) -> p s j i", i=NEIGHBOURS),
             )
             codes = keep.tile([P, n], U32, name=f"codes{c}_{a}", tag=codes_tag, align_bytes=64)
-            plane = keep.tile([P, n], U8, name=f"plane{c}_{a}", align_bytes=64)
+            scale_rows = keep.tile([P, n], U8, name=f"scale_rows{c}_{a}", align_bytes=64)
             nc.vector.quantize_mx(
-                out=codes[:].bitcast(FP8X4), scales=plane[:], in_=grouped[:].rearrange("p s j -> p (s j)")
+                out=codes[:].bitcast(FP8X4), scales=scale_rows[:], in_=grouped[:].rearrange("p s j -> p (s j)")
             )
-            quantised[c, a] = codes, plane
+            quantised[c, a] = codes, scale_rows
 
         def multiply(c, a, m):
-            codes, plane = quantised[c, a]
+            codes, scale_rows = quantised[c, a]
             if a == 0:
                 acc[c, m] = psum.tile([P, CHUNKS[c][1]], F32, name=f"acc{m}")
             nc.tensor.matmul_mx(
                 out=acc[c, m][:],
-                lhsT=w_block(a, m),
-                lhsT_scale=w_planes[4 * a : P, m * P : (m + 1) * P],
+                lhsT=w_codes[a, m].bitcast(FP8X4),
+                lhsT_scale=w_scale_rows[a * SCALE_ROWS : P, m * P : (m + 1) * P],
                 rhs=codes[:].bitcast(FP8X4),
-                rhs_scale=plane[:],
+                rhs_scale=scale_rows[:],
                 start=(a == 0),
                 stop=(a == PASSES - 1),
             )
 
-        def place(c, m, tag):
-            c0, n = CHUNKS[c]
-            y = keep.tile([P, n], F32, name=f"y{c}_{m}", tag=tag, align_bytes=64)
+        def place(c, m, y_tag):
+            start, n = CHUNKS[c]
+            y = keep.tile([P, n], F32, name=f"y{c}_{m}", tag=y_tag, align_bytes=64)
             nc.scalar.activation(y[:], acc[c, m][:], RELU, bias=bias[:, m : m + 1])
-            nc.vector.tensor_tensor(
-                windows[m][:].indirect(offsets[:, c0 // 16 : (c0 + n) // 16]), y[:], gate_of(c, m), MULT
-            )
-            if c == len(CHUNKS) - 1:
+            listed = windows[m][:].indirect(offsets[:, start // LIST_ROWS : (start + n) // LIST_ROWS])
+            nc.vector.tensor_tensor(listed, y[:], gates[c, m], MULT)
+            if c == LAST:
                 nc.sync.dma_start(out=out[m * P : (m + 1) * P, :], in_=windows[m][:])
 
         for a in range(PASSES):
@@ -159,6 +157,7 @@ def tile_picked_place_lin_relu_sub_l_kernel(tc, xT, w_words, w_scales, b, gate, 
         nc.vector.memset(windows[2][:], 0.0)
         for m in range(3):
             place(0, m, f"y0_{m}")
+
         for a in range(PASSES):
             quantise(1, a, f"codes0_{a}", f"codes1_{a}")
         for m in range(BLOCKS):
@@ -167,8 +166,9 @@ def tile_picked_place_lin_relu_sub_l_kernel(tc, xT, w_words, w_scales, b, gate, 
         place(0, 3, "raw1_1")
         for m in (0, 1):
             place(1, m, f"y1_{m}")
+
         for a in range(PASSES):
-            quantise(2, a, f"codes1_{a}", f"codes2_{a}")
+            quantise(2, a, "codes1_0", f"codes2_{a}")
             for m in range(BLOCKS):
                 multiply(2, a, m)
             place(1, 2 + a, f"raw2_{a}")

from contextlib import ExitStack

import concourse.mybir as mybir
from concourse.masks import make_identity

K, T, S, N = 1024, 1024, 512, 512
FLOPS = 2 * K * S * N

F32 = mybir.dt.float32
BF16 = mybir.dt.bfloat16
I32 = mybir.dt.int32
U32 = mybir.dt.uint32
U16 = mybir.dt.uint16
U8 = mybir.dt.uint8
FP8X4 = mybir.dt.float8_e4m3fn_x4
RELU = mybir.ActivationFunctionType.Relu
MULT = mybir.AluOpType.mult

P = 128
PACK = 4
K_PASS = P * PACK
PASSES = K // K_PASS
BLOCKS = N // P
QUADRANTS = 4
SCALE_ROWS = 4
LIST_ROWS = 16
NEIGHBOURS = 4

CHUNKS = ((0, 128), (128, 128), (256, 256))
LAST = len(CHUNKS) - 1
HALVES = ((0, 2), (2, 4))
GATE_PARTS = (HALVES, ((0, 4),), ((0, 4),))


def tile_picked_place_lin_relu_sub_l_kernel(tc, xT, w_words, w_scales, b, gate, offs, out):
    nc = tc.nc
    with ExitStack() as ctx:
        lists = ctx.enter_context(tc.tile_pool(name="lists", bufs=1))
        keep = ctx.enter_context(tc.tile_pool(name="keep", bufs=1))
        psum = ctx.enter_context(tc.psum_pool(name="psum", bufs=2))

        offsets = lists.tile([P, S // LIST_ROWS], U16, name="offsets")
        w_scale_rows = keep.tile([P, N], U8, name="w_scale_rows", align_bytes=64)
        bias_rows = keep.tile([P, P], F32, name="bias_rows")
        identity = keep.tile([P, P], F32, name="identity")
        bias = keep.tile([P, BLOCKS], F32, name="bias")
        first_relu = keep.tile([P, 1], F32, name="first_relu")
        windows = {m: keep.tile([P, T], F32, name=f"window{m}") for m in (0, 1, 3)}
        w_codes = {}
        gates = {}
        raw = {}
        quantised = {}
        acc = {}

        def load_x(c, a):
            start, n = CHUNKS[c]
            rows = xT[a * K_PASS : (a + 1) * K_PASS, start : start + n]
            raw[c, a] = keep.tile([P, PACK, n], F32, name=f"raw{c}_{a}", tag=f"raw{c}_{a}", align_bytes=64)
            nc.sync.dma_start(out=raw[c, a][:], in_=rows.rearrange("(p j) s -> p j s", j=PACK))

        def load_w(lo, hi):
            words = keep.tile([P, PASSES, (hi - lo) * P], U32, name=f"w_codes{lo}", align_bytes=64)
            part = w_words[:, :, lo * P : hi * P, :].rearrange("a p m r -> p a (m r)")
            nc.sync.dma_start(out=words[:].bitcast(I32), in_=part.bitcast(I32))
            for a in range(PASSES):
                for m in range(lo, hi):
                    w_codes[a, m] = words[:, a, (m - lo) * P : (m - lo + 1) * P]

        def load_w_scales(q):
            rows = w_scales[:, q * SCALE_ROWS : (q + 1) * SCALE_ROWS, :]
            first = q * (P // QUADRANTS)
            nc.sync.dma_start(
                out=w_scale_rows[first : first + PASSES * SCALE_ROWS, :].bitcast(I32), in_=rows.bitcast(I32)
            )

        def load_gate(c, lo, hi):
            start, n = CHUNKS[c]
            part = keep.tile([P, hi - lo, n], F32, name=f"gate{c}_{lo}")
            rows = gate[lo * P : hi * P, start : start + n]
            nc.sync.dma_start(out=part[:], in_=rows.rearrange("(m p) s -> p m s", p=P))
            for m in range(lo, hi):
                gates[c, m] = part[:, m - lo, :]

        nc.gpsimd.memset(w_scale_rows[:].bitcast(I32), 0)
        nc.vector.memset(first_relu[:], 0.0)
        nc.scalar.activation(first_relu[:], first_relu[:], RELU)
        nc.gpsimd.memset(bias_rows[:], 0.0)
        nc.gpsimd.dma_start(out=bias_rows[0:BLOCKS, :], in_=b.rearrange("(m p) o -> m (p o)", p=P))
        make_identity(nc, identity[:])

        for a in range(PASSES):
            load_x(0, a)
        for q in range(QUADRANTS):
            load_w_scales(q)
        load_w(*HALVES[0])
        load_gate(0, *HALVES[0])
        nc.sync.dma_start(offsets[:], offs)
        load_w(*HALVES[1])
        load_gate(0, *HALVES[1])
        for c in range(1, len(CHUNKS)):
            for a in range(PASSES):
                load_x(c, a)
            for lo, hi in GATE_PARTS[c]:
                load_gate(c, lo, hi)

        for m in (0, 1):
            nc.vector.memset(windows[m][:], 0.0)
        nc.gpsimd.memset(windows[3][:], 0.0)

        def quantise(c, a, grouped_tag, codes_tag):
            n = CHUNKS[c][1]
            grouped = keep.tile([P, n, PACK], BF16, name=f"grouped{c}_{a}", tag=grouped_tag, align_bytes=64)
            copy = nc.vector.tensor_copy if c == 0 else nc.scalar.copy
            copy(
                out=grouped[:].rearrange("p (s i) j -> p s j i", i=NEIGHBOURS),
                in_=raw[c, a][:].rearrange("p j (s i) -> p s j i", i=NEIGHBOURS),
            )
            codes = keep.tile([P, n], U32, name=f"codes{c}_{a}", tag=codes_tag, align_bytes=64)
            scale_rows = keep.tile([P, n], U8, name=f"scale_rows{c}_{a}", align_bytes=64)
            nc.vector.quantize_mx(
                out=codes[:].bitcast(FP8X4), scales=scale_rows[:], in_=grouped[:].rearrange("p s j -> p (s j)")
            )
            quantised[c, a] = codes, scale_rows

        def multiply(c, a, m):
            codes, scale_rows = quantised[c, a]
            if a == 0:
                acc[c, m] = psum.tile([P, CHUNKS[c][1]], F32, name=f"acc{m}")
            nc.tensor.matmul_mx(
                out=acc[c, m][:],
                lhsT=w_codes[a, m].bitcast(FP8X4),
                lhsT_scale=w_scale_rows[a * SCALE_ROWS : P, m * P : (m + 1) * P],
                rhs=codes[:].bitcast(FP8X4),
                rhs_scale=scale_rows[:],
                start=(a == 0),
                stop=(a == PASSES - 1),
            )

        def place(c, m, y_tag):
            start, n = CHUNKS[c]
            y = keep.tile([P, n], F32, name=f"y{c}_{m}", tag=y_tag, align_bytes=64)
            nc.scalar.activation(y[:], acc[c, m][:], RELU, bias=bias[:, m : m + 1])
            listed = windows[m][:].indirect(offsets[:, start // LIST_ROWS : (start + n) // LIST_ROWS])
            nc.vector.tensor_tensor(listed, y[:], gates[c, m], MULT)
            if c == LAST:
                nc.sync.dma_start(out=out[m * P : (m + 1) * P, :], in_=windows[m][:])

        for a in range(PASSES):
            quantise(0, a, f"grouped0_{a}", f"codes0_{a}")
        turned = psum.tile([P, P], F32, name="turned", tag="acc3")
        nc.tensor.transpose(turned[:], bias_rows[:], identity[:])
        nc.scalar.copy(out=bias[:], in_=turned[:, 0:BLOCKS])
        for m in range(BLOCKS):
            for a in range(PASSES):
                multiply(0, a, m)
        windows[2] = keep.tile([P, T], F32, name="window2", tag="grouped0_1", align_bytes=64)
        nc.vector.memset(windows[2][:], 0.0)
        for m in range(3):
            place(0, m, f"y0_{m}")

        for a in range(PASSES):
            quantise(1, a, f"codes0_{a}", f"codes1_{a}")
        for m in range(BLOCKS):
            for a in range(PASSES):
                multiply(1, a, m)
        place(0, 3, "raw1_1")
        for m in (0, 1):
            place(1, m, f"y1_{m}")

        for a in range(PASSES):
            quantise(2, a, "codes1_0", f"codes2_{a}")
            for m in range(BLOCKS):
                multiply(2, a, m)
            place(1, 2 + a, f"raw2_{a}")
        for m in range(BLOCKS):
            place(2, m, f"y2_{m}")
